import numpy as np
import ml_dtypes


def mxq(x, axis, fmt="e4m3"):
    dtype, down = {"e4m3": (ml_dtypes.float8_e4m3fn, 7), "e5m2": (ml_dtypes.float8_e5m2, 14)}[fmt]
    v = np.moveaxis(np.asarray(x, np.float32).astype(ml_dtypes.bfloat16).astype(np.float64), axis, -1)
    blocks = v.reshape(v.shape[:-1] + (-1, 32))
    amax = np.abs(blocks).max(-1, keepdims=True)
    byte = np.maximum(np.where(amax > 0, np.frexp(amax)[1] - 1 + 127, 0) - down, 1)
    scale = np.exp2(byte - 127.0)
    codes = (blocks / scale).astype(np.float32).astype(dtype).astype(np.float64)
    return np.moveaxis((codes * scale).reshape(v.shape), -1, axis)


WIDE = False


def mx_kscale(k):
    if not WIDE:
        return np.ones(k)
    levels = np.array([10, -10, 5, -5, 0])
    if k % 512:
        return np.exp2(np.random.permutation(np.resize(levels, k // 32))).repeat(32)
    a = np.empty((k // 512, 16))
    for p in range(k // 512):
        a[p, :8] = np.random.permutation(np.resize(levels, 8))
        for g in range(8):
            far = levels[np.abs(levels - a[p, g]) >= 10]
            a[p, g + 8] = far[np.random.randint(len(far))]
    return np.exp2(a.ravel()).repeat(32)


BF16 = ml_dtypes.bfloat16


def bf(x):
    return np.asarray(x, np.float32).astype(BF16)


def f64(x):
    return np.asarray(x).astype(np.float64)

def planes(Y):
    n, m = Y.shape
    b = f64(bf(Y)).reshape(n // 32, 32, m)
    amax = np.abs(b).max(1)
    byte = np.clip(np.where(amax > 0, np.frexp(amax)[1] - 1 + 127 - 7, 1), 1, 254)
    codes = (b * np.exp2(127.0 - byte)[:, None, :]).reshape(n, m).astype(np.float32).astype(ml_dtypes.float8_e4m3fn).view(np.uint8)
    words = codes.reshape(n // 512, 128, 4, m).transpose(0, 1, 3, 2)
    return np.ascontiguousarray(words), np.ascontiguousarray(byte.astype(np.uint8).reshape(n // 512, 16, m))


ITEMS, D, USERS = 1536, 1024, 1024


def setup_inputs():
    s = mx_kscale(ITEMS)
    t = mx_kscale(ITEMS)
    sim = np.random.randn(ITEMS, ITEMS) / np.sqrt(ITEMS) * s[None, :]
    side = np.random.randn(ITEMS, D) / s[:, None]
    factor_w = np.random.randn(ITEMS, D) * t[:, None]
    history = np.random.randn(USERS, ITEMS) / np.sqrt(ITEMS) / t[None, :]
    return {
        "sim": bf(sim),
        "side": bf(side),
        "factor_w": bf(factor_w),
        "history": bf(history),
        "user_base": bf(0.5 * np.random.randn(USERS, D)),
        "user_scale": bf(1 + 0.1 * np.random.randn(USERS)),
        "factor_gain": bf(np.exp(0.7 * np.random.randn(D))),
    }

def reference(sim, side, factor_w, history, user_base, user_scale, factor_gain):
    a = mxq(f64(sim), 1, "e4m3") @ mxq(f64(side), 0, "e4m3")
    z = np.maximum(a, 0.0) * f64(factor_w)
    h = mxq(f64(history), 1, "e4m3") @ mxq(z, 0, "e4m3")
    y = (f64(user_base) + f64(user_scale)[:, None] * h) * f64(factor_gain)[None, :]
    Y = y.T
    words, scales = planes(Y)
    return y, words, scales

@@ -1,0 +1,523 @@
+from contextlib import ExitStack
+
+import concourse.mybir as mybir
+from concourse.masks import make_identity
+
+ITEMS, D, USERS = 1536, 1024, 1024
+FLOPS = 2 * ITEMS * ITEMS * D + 2 * USERS * ITEMS * D
+
+F32 = mybir.dt.float32
+BF16 = mybir.dt.bfloat16
+U32 = mybir.dt.uint32
+I32 = mybir.dt.int32
+U8 = mybir.dt.uint8
+FP8X4 = mybir.dt.float8_e4m3fn_x4
+ALU = mybir.AluOpType
+
+P = 128
+PASSES = ITEMS // 512
+HALF = 512
+QUARTER = 256
+PAIRS = USERS // (2 * P)
+G_MULT = False
+G_BOTH = False
+PRESORT = ()
+RING = 8
+SIDE_V_COLS = 256
+SIDE1_V_COLS = 192
+YLAG = 2
+
+
+def tile_item_history_factors_h3_kernel(
+    tc, sim, side, factor_w, history, user_base, user_scale, factor_gain, out_0, out_1, out_2
+):
+    nc = tc.nc
+    with ExitStack() as ctx:
+        keep = ctx.enter_context(tc.tile_pool(name="keep", bufs=1))
+        stage = ctx.enter_context(tc.tile_pool(name="stage", bufs=1))
+        psum = ctx.enter_context(tc.psum_pool(name="psum", bufs=1))
+        ctx.enter_context(tc.manual_schedule(engines={mybir.EngineType.PE, mybir.EngineType.SP}))
+
+        banks_taken = []
+
+        def next_bank(shape, dtype):
+            n = len(banks_taken)
+            banks_taken.append(n)
+            return psum.tile(shape, dtype, name="bank%d" % n, tag="bank%d" % (n % RING))
+
+        ident32 = keep.tile([P, P], F32, name="ident32")
+        ident16 = keep.tile([P, P], BF16, name="ident16")
+        vec_rows = keep.tile([P, P], BF16, name="vec_rows")
+        nc.gpsimd.memset(vec_rows[:], 0.0)
+        make_identity(nc, ident32[:])
+        make_identity(nc, ident16[:])
+
+        rows = {}
+        side_raw = {}
+        w_raw = {}
+        base_raw = {}
+
+        def load_sim(g, t):
+            r = keep.tile([P, ITEMS], BF16, name="sim%d_%d" % (g, t), tag="rows%d" % (4 * g + t))
+            nc.sync.dma_start(
+                out=r[:], in_=sim[512 * g : 512 * (g + 1), :].rearrange("(m t) k -> m t k", t=4)[:, t, :]
+            )
+            rows["sim", 4 * g + t] = r
+
+        def load_hist(v):
+            r = keep.tile([P, ITEMS], BF16, name="hist%d" % v, tag="rows%d" % v)
+            nc.sync.dma_start(out=r[:], in_=history[P * v : P * (v + 1), :])
+            rows["hist", v] = r
+
+        def load_k_first(src, store, label, g, h):
+            slot = ("side", g, 0) if (label, h) == ("w", 1) else (label, g, h)
+            r = keep.tile([P, 4, HALF], BF16, name="%s%d_%d" % (label, g, h), tag="%s%d_%d" % slot)
+            nc.sync.dma_start(
+                out=r[:],
+                in_=src[512 * g : 512 * (g + 1), HALF * h : HALF * (h + 1)].rearrange("(p j) n -> p j n", j=4),
+            )
+            store[g, h] = r
+
+        def load_side(h):
+            for c in range(PASSES):
+                load_k_first(side, side_raw, "side", c, h)
+
+        def load_w(g, h):
+            load_k_first(factor_w, w_raw, "w", g, h)
+
+        def load_base(pr):
+            r = keep.tile([P, 2, D], BF16, name="base%d" % pr)
+            nc.sync.dma_start(
+                out=r[:], in_=user_base[2 * P * pr : 2 * P * (pr + 1), :].rearrange("(v p) d -> p v d", p=P)
+            )
+            base_raw[pr] = r
+
+        turned = {}
+
+        presorted = []
+
+        def presort(kind, r):
+            if (kind, r) not in PRESORT:
+                return
+            s = keep.tile([P, ITEMS], BF16, name="sorted%d" % r, tag="rows%d" % (8 + len(presorted) % 4))
+            nc.scalar.copy(
+                out=s[:].bitcast(F32).rearrange("p (c u q) -> p c u q", c=PASSES, u=2),
+                in_=rows[kind, r][:].bitcast(F32).rearrange("p (c q u) -> p c u q", c=PASSES, u=2),
+            )
+            rows[kind, r] = s
+            presorted.append((kind, r))
+
+        def turn_bank(kind, a, j):
+            units = [(a, 0), (a, 1), (a, 2), (a + 1, 0), (a + 1, 1), (a + 1, 2)][2 * j : 2 * j + 2]
+            bank = next_bank([P, 2, 2, P], F32)
+            for s, (r, c) in enumerate(units):
+                words = rows[kind, r][:].bitcast(F32)
+                for u in range(2):
+                    if (kind, r) in presorted:
+                        src = words[:, 256 * c + P * u : 256 * c + P * (u + 1)]
+                    else:
+                        src = words[:, 256 * c + u : 256 * (c + 1) : 2]
+                    nc.tensor.transpose(bank[:, s, u, :], src, ident32[:])
+            return bank, units
+
+        def turn_exit(bank):
+            st = stage.tile([P, 2 * P * 4], BF16, name="turn_stage", bufs=5, align_bytes=64)
+            nc.scalar.copy(
+                out=st[:].bitcast(F32).rearrange("p (s m u) -> p s m u", s=2, u=2),
+                in_=bank[:].rearrange("p s u m -> p s m u"),
+            )
+            return st
+
+        def turn_quant(kind, units, st):
+            label = "%s%d_%d" % (kind, units[0][0], units[0][1])
+            codes = keep.tile([P, 2 * P], U32, name="tc_" + label, align_bytes=64)
+            scales = keep.tile([P, 2 * P], U8, name="ts_" + label, align_bytes=64)
+            nc.vector.quantize_mx(out=codes[:].bitcast(FP8X4), scales=scales[:], in_=st[:])
+            for s, (r, c) in enumerate(units):
+                turned[kind, r, c] = (codes[:, P * s : P * (s + 1)], scales[:, P * s : P * (s + 1)])
+
+        def turn_run(kind, a):
+            staged = []
+            for j in range(3):
+                bank, units = turn_bank(kind, a, j)
+                staged.append((units, turn_exit(bank)))
+            return staged
+
+        moving = {}
+
+        def wide_quant(kind, c, h, grouped):
+            codes = keep.tile([P, HALF], U32, name="mc_%s%d_%d" % (kind, c, h), align_bytes=64)
+            scales = keep.tile([P, HALF], U8, name="ms_%s%d_%d" % (kind, c, h), align_bytes=64)
+            nc.vector.quantize_mx(out=codes[:].bitcast(FP8X4), scales=scales[:], in_=grouped[:])
+            moving[kind, c, h] = (codes, scales)
+
+        def side_group(c, h, v_cols):
+            grouped = stage.tile([P, HALF * 4], BF16, name="grouped", bufs=3, align_bytes=64)
+            dst = grouped[:].rearrange("p (c i t) -> p c t i", i=4, t=4)
+            src = side_raw[c, h][:].rearrange("p t (c i) -> p c t i", i=4)
+            cut = v_cols // 4
+            if cut > 0:
+                nc.vector.tensor_copy(out=dst[:, :cut], in_=src[:, :cut])
+            if cut < HALF // 4:
+                nc.scalar.copy(out=dst[:, cut:], in_=src[:, cut:])
+            return grouped
+
+        def a_pass(bank, g, h, u, q, e, c):
+            lc, ls = turned["sim", 4 * g + 2 * u + e, c]
+            rc, rs = moving["side", c, h]
+            cols = slice(QUARTER * q, QUARTER * (q + 1))
+            nc.tensor.matmul_mx(
+                out=bank[:, e, :], lhsT=lc.bitcast(FP8X4), lhsT_scale=ls,
+                rhs=rc[:, cols].bitcast(FP8X4), rhs_scale=rs[:, cols],
+                start=(c == 0), stop=(c == PASSES - 1),
+            )
+
+        def a_exit(bank, g, h, u, q, zpair):
+            cols = slice(QUARTER * q, QUARTER * (q + 1))
+            nc.vector.scalar_tensor_tensor(
+                out=zpair[:, u, 2 * QUARTER * q : 2 * QUARTER * (q + 1)].rearrange("p (n e) -> p n e", e=2),
+                in0=bank[:].rearrange("p e n -> p n e"),
+                scalar=0.0,
+                in1=w_raw[g, h][:, 2 * u : 2 * u + 2, cols].rearrange("p e n -> p n e"),
+                op0=ALU.max, op1=ALU.mult,
+            )
+
+        def new_zpair():
+            return stage.tile([P, 2, 2 * HALF], BF16, name="zpair", bufs=2)
+
+        def a_bank(g, h, u, q, zpair):
+            bank = next_bank([P, 2, QUARTER], F32)
+            for e in range(2):
+                for c in range(PASSES):
+                    a_pass(bank, g, h, u, q, e, c)
+            a_exit(bank, g, h, u, q, zpair)
+
+        def z_group(zpair):
+            grouped = stage.tile([P, HALF * 4], BF16, name="grouped", bufs=3, align_bytes=64)
+            nc.scalar.copy(
+                out=grouped[:].bitcast(F32).rearrange("p (n u) -> p n u", u=2),
+                in_=zpair[:].bitcast(F32).rearrange("p u n -> p n u"),
+            )
+            return grouped
+
+        BANK_ORDER = [(0, 0), (0, 1), (1, 0), (1, 1)]
+
+        def a_half(g, h, u, zpair, between=()):
+            a_bank(g, h, u, 0, zpair)
+            for f in between:
+                f()
+            a_bank(g, h, u, 1, zpair)
+
+        def quant_later(kind, staged, j):
+            return lambda: turn_quant(kind, staged[j][0], staged[j][1])
+
+        def quants(kind, staged):
+            return [quant_later(kind, staged, j) for j in range(3)]
+
+        def zq_later(g, h, grouped):
+            return lambda: wide_quant("z", g, h, grouped)
+
+        y_scales = keep.tile([P, 2, USERS], U8, name="y_scales", align_bytes=64)
+        words_out = out_1.rearrange("g p m t -> g p (m t)").bitcast(I32)
+        gain_cols = keep.tile([P, 8], BF16, name="gain_cols")
+        scale_cols = keep.tile([P, 8], F32, name="scale_cols")
+        gain = keep.tile([P, D], BF16, name="gain")
+
+        gain_src = []
+
+        def h_bank(v, h):
+            bank = next_bank([P, HALF], F32)
+            for c in range(PASSES):
+                lc, ls = turned["hist", v, c]
+                rc, rs = moving["z", c, h]
+                nc.tensor.matmul_mx(
+                    out=bank[:], lhsT=lc.bitcast(FP8X4), lhsT_scale=ls,
+                    rhs=rc[:].bitcast(FP8X4), rhs_scale=rs[:],
+                    start=(c == 0), stop=(c == PASSES - 1),
+                )
+            s = stage.tile([P, HALF], F32, name="sums", bufs=4)
+            nc.vector.scalar_tensor_tensor(
+                out=s[:], in0=bank[:], scalar=scale_cols[:, v : v + 1],
+                in1=base_raw[v // 2][:, v % 2, HALF * h : HALF * (h + 1)], op0=ALU.mult, op1=ALU.add,
+            )
+            return s
+
+        def y_mult(h, s, y, on_gpsimd):
+            cols = slice(HALF * h, HALF * (h + 1))
+            if on_gpsimd:
+                nc.gpsimd.tensor_tensor(out=y, in0=s[:], in1=gain[:, cols], op=ALU.mult)
+            else:
+                nc.vector.tensor_tensor(out=y, in0=s[:], in1=gain_src[0][:, cols], op=ALU.mult)
+
+        def y_round(y, ysort):
+            nc.scalar.copy(
+                out=ysort.rearrange("p (u q e) -> p u q e", u=2, e=2),
+                in_=y.rearrange("p (q u e) -> p u q e", u=2, e=2),
+            )
+
+        def h_step(pr, h, mid=(), between=(), last=False):
+            cols = slice(HALF * h, HALF * (h + 1))
+            y = stage.tile([P, 2, HALF], F32, name="y", bufs=4)
+            dst = out_0[2 * P * pr : 2 * P * (pr + 1), cols].rearrange("(v p) d -> p v d", p=P)
+            ysorts = []
+            for v in range(2):
+                ysorts.append(stage.tile([P, HALF], BF16, name="ysort", bufs=8))
+            s0 = h_bank(2 * pr, h)
+            first_on_gpsimd = G_MULT and not (last and G_BOTH)
+            if first_on_gpsimd:
+                y_mult(h, s0, y[:, 0, :], True)
+            owed = [f() for f in mid]
+            s1 = h_bank(2 * pr + 1, h)
+            if not first_on_gpsimd:
+                y_mult(h, s0, y[:, 0, :], False)
+            if last:
+                y_round(y[:, 0, :], ysorts[0][:])
+                nc.sync.dma_start(out=dst[:, 0, :], in_=y[:, 0, :])
+                nc.vector.tensor_tensor(
+                    out=ysorts[1][:].rearrange("p (u q e) -> p u q e", u=2, e=2),
+                    in0=s1[:].rearrange("p (q u e) -> p u q e", u=2, e=2),
+                    in1=gain_src[0][:, cols].rearrange("p (q u e) -> p u q e", u=2, e=2),
+                    op=ALU.mult,
+                )
+                ylast = stage.tile([P, 2, HALF], F32, name="y", bufs=4)
+                y_mult(h, s1, ylast[:, 1, :], False)
+                nc.sync.dma_start(out=dst[:, 1, :], in_=ylast[:, 1, :])
+            else:
+                y_mult(h, s1, y[:, 1, :], G_BOTH)
+                for v in range(2):
+                    y_round(y[:, v, :], ysorts[v][:])
+                nc.sync.dma_start(out=dst, in_=y[:])
+            for f in list(between) + [f for f in owed if f]:
+                f()
+            return ysorts
+
+        def y_turn(first_tile, h, ysorts):
+            n = len(ysorts)
+            bank = next_bank([P, n, 2, P], F32)
+            for s in range(n):
+                words = ysorts[s][:].bitcast(F32)
+                for u in range(2):
+                    nc.tensor.transpose(bank[:, s, u, :], words[:, P * u : P * (u + 1)], ident32[:])
+            st = stage.tile([P, n * P * 4], BF16, name="turn_stage", bufs=5, align_bytes=64)
+            nc.scalar.copy(
+                out=st[:].bitcast(F32).rearrange("p (s m u) -> p s m u", s=n, u=2),
+                in_=bank[:].rearrange("p s u m -> p s m u"),
+            )
+            return lambda: y_quant(first_tile, n, h, st)
+
+        def y_quant(first_tile, n, h, st):
+            users = slice(P * first_tile, P * (first_tile + n))
+            codes = stage.tile([P, n * P], U32, name="y_codes", bufs=5, align_bytes=64)
+            nc.vector.quantize_mx(out=codes[:].bitcast(FP8X4), scales=y_scales[:, h, users], in_=st[:])
+            nc.sync.dma_start(out=words_out[h, :, users], in_=codes[:].bitcast(I32))
+
+        def store_scales():
+            scales_out = out_2.bitcast(I32)
+            for quad in range(4):
+                nc.sync.dma_start(
+                    out=scales_out[:, 4 * quad : 4 * quad + 4, :].rearrange("g r m -> r g m"),
+                    in_=y_scales[32 * quad : 32 * quad + 4, :, :].bitcast(I32),
+                )
+
+        def z_quarter(g, h, q, zpair):
+            if q == 0:
+                codes = keep.tile([P, HALF], U32, name="mc_z%d_%d" % (g, h), align_bytes=64)
+                scales = keep.tile([P, HALF], U8, name="ms_z%d_%d" % (g, h), align_bytes=64)
+                moving["z", g, h] = (codes, scales)
+            codes, scales = moving["z", g, h]
+            cols = slice(QUARTER * q, QUARTER * (q + 1))
+            st = stage.tile([P, 2 * P * 4], BF16, name="turn_stage", bufs=5, align_bytes=64)
+            nc.scalar.copy(
+                out=st[:].bitcast(F32).rearrange("p (n u) -> p n u", u=2),
+                in_=zpair[:].bitcast(F32).rearrange("p u n -> p n u"),
+            )
+            return lambda: nc.vector.quantize_mx(
+                out=codes[:, cols].bitcast(FP8X4), scales=scales[:, cols], in_=st[:]
+            )
+
+        def a_quarter(g, h, q, between=()):
+            zpair = stage.tile([P, 2, HALF], BF16, name="zquarter", bufs=2)
+            cols = slice(QUARTER * q, QUARTER * (q + 1))
+            for u in range(2):
+                bank = next_bank([P, 2, QUARTER], F32)
+                for e in range(2):
+                    for c in range(PASSES):
+                        a_pass(bank, g, h, u, q, e, c)
+                nc.vector.scalar_tensor_tensor(
+                    out=zpair[:, u, :].rearrange("p (n e) -> p n e", e=2),
+                    in0=bank[:].rearrange("p e n -> p n e"),
+                    scalar=0.0,
+                    in1=w_raw[g, h][:, 2 * u : 2 * u + 2, cols].rearrange("p e n -> p n e"),
+                    op0=ALU.max, op1=ALU.mult,
+                )
+                if u == 0:
+                    for f in between:
+                        f()
+            return z_quarter(g, h, q, zpair)
+
+        def side_quarters(c):
+            codes = keep.tile([P, HALF], U32, name="mc_side%d_0" % c, align_bytes=64)
+            scales = keep.tile([P, HALF], U8, name="ms_side%d_0" % c, align_bytes=64)
+            moving["side", c, 0] = (codes, scales)
+            src = side_raw[c, 0][:].rearrange("p t (c i) -> p c t i", i=4)
+            calls = []
+            for q, copy in enumerate((nc.vector.tensor_copy, nc.scalar.copy)):
+                st = stage.tile([P, 2 * P * 4], BF16, name="turn_stage", bufs=5, align_bytes=64)
+                copy(out=st[:].rearrange("p (c i t) -> p c t i", i=4, t=4), in_=src[:, 64 * q : 64 * (q + 1)])
+                cols = slice(QUARTER * q, QUARTER * (q + 1))
+                calls.append(
+                    lambda cols=cols, st=st: nc.vector.quantize_mx(
+                        out=codes[:, cols].bitcast(FP8X4), scales=scales[:, cols], in_=st[:]
+                    )
+                )
+            return calls
+
+        def make_gain():
+            if RING == 7:
+                gbank = psum.tile([P, D], BF16, name="gbank")
+            else:
+                gbank = psum.tile([P, D], BF16, name="gbank", tag="bank7")
+            for c in range(8):
+                nc.tensor.transpose(
+                    gbank[:, P * c : P * (c + 1)], gain_cols[:, c : c + 1].to_broadcast([P, P]), ident16[:]
+                )
+            gain_src.append(gbank if RING == 7 else gain)
+            return gbank
+
+        for t in range(4):
+            load_sim(0, t)
+        nc.sync.dma_start(out=vec_rows[0:8, :], in_=factor_gain.rearrange("(c p) -> c p", p=P))
+        nc.sync.dma_start(out=vec_rows[8:16, :], in_=user_scale.rearrange("(c p) -> c p", p=P))
+        load_side(0)
+        load_sim(1, 0)
+        load_sim(1, 1)
+        load_w(0, 0)
+        load_sim(1, 2)
+        load_sim(1, 3)
+        load_w(1, 0)
+        load_sim(2, 0)
+        load_sim(2, 1)
+        load_k_first(side, side_raw, "side", 0, 1)
+        load_sim(2, 2)
+        load_sim(2, 3)
+        load_k_first(side, side_raw, "side", 1, 1)
+        load_w(2, 0)
+        load_k_first(side, side_raw, "side", 2, 1)
+
+        with tc.manual_schedule():
+            for f in quants("sim", turn_run("sim", 0)):
+                f()
+            late = quants("sim", turn_run("sim", 2))
+            vbank = next_bank([P, P], BF16)
+            nc.tensor.transpose(vbank[:], vec_rows[:], ident16[:])
+            late[0]()
+            nc.vector.tensor_copy(out=gain_cols[:], in_=vbank[:, 0:8])
+            nc.vector.tensor_copy(out=scale_cols[:], in_=vbank[:, 8:16])
+            late[1]()
+            gbank = make_gain()
+
+            load_hist(0)
+            load_hist(1)
+
+            zp = new_zpair()
+            first = {}
+            for u, q in BANK_ORDER:
+                first[u, q] = next_bank([P, 2, QUARTER], F32)
+            owed = late[2]
+            for c in range(PASSES):
+                sq = side_quarters(c)
+                owed()
+                if c > 0 and c < PASSES:
+                    for u in range(2):
+                        a_pass(first[u, 1], 0, 0, u, 1, 0, c - 1)
+                sq[0]()
+                owed = sq[1]
+                if c == PASSES - 1:
+                    owed()
+                    nc.scalar.copy(out=gain[:], in_=gbank[:])
+                    late = quants("sim", turn_run("sim", 4))
+                for u in range(2):
+                    a_pass(first[u, 0], 0, 0, u, 0, 0, c)
+            for u in range(2):
+                a_pass(first[u, 1], 0, 0, u, 1, 0, PASSES - 1)
+            for f in late:
+                f()
+            for u, q in BANK_ORDER:
+                for c in range(PASSES):
+                    a_pass(first[u, q], 0, 0, u, q, 1, c)
+                a_exit(first[u, q], 0, 0, u, q, zp)
+        late = quants("sim", turn_run("sim", 6))
+
+        load_w(0, 1)
+        load_base(0)
+        load_hist(2)
+        load_hist(3)
+        load_base(1)
+        load_hist(4)
+        load_hist(5)
+        load_w(1, 1)
+        load_base(2)
+        load_hist(6)
+        load_hist(7)
+        load_w(2, 1)
+        load_base(3)
+
+        zq = zq_later(0, 0, z_group(zp))
+        zp = new_zpair()
+        for f in late:
+            f()
+        a_half(1, 0, 0, zp)
+        zq()
+        late = quants("sim", turn_run("sim", 8))
+        sg0 = side_group(0, 1, SIDE1_V_COLS)
+        late[0]()
+        late[1]()
+        a_half(1, 0, 1, zp, late[2:])
+        late = quants("sim", turn_run("sim", 10))
+        wide_quant("side", 0, 1, sg0)
+        sg1 = side_group(1, 1, SIDE1_V_COLS)
+        zq = zq_later(1, 0, z_group(zp))
+        zp = new_zpair()
+        late[0]()
+        late[1]()
+        a_half(2, 0, 0, zp, late[2:])
+        sg2 = side_group(2, 1, SIDE1_V_COLS)
+        wide_quant("side", 1, 1, sg1)
+        a_half(2, 0, 1, zp, [zq])
+        wide_quant("side", 2, 1, sg2)
+
+        quarters = [(g, q) for g in range(PASSES) for q in range(2)]
+        owed = zq_later(2, 0, z_group(zp))
+        pend = []
+        for pr in range(PAIRS):
+            late = quants("hist", turn_run("hist", 2 * pr))
+            yq = []
+            if pr >= 2:
+                yq = [y_turn(*pend[0])]
+                pend = pend[1:]
+            if pr < PAIRS - 1:
+                presort("hist", 2 * pr + 2)
+                presort("hist", 2 * pr + 3)
+            owed()
+            late[0]()
+            owed = a_quarter(quarters[pr][0], 1, quarters[pr][1], late[1:])
+            if pr == PAIRS - 1:
+                for f in yq:
+                    f()
+                nxt = a_quarter(2, 1, 0, [owed])
+                owed = a_quarter(2, 1, 1, [nxt])
+                yq = [y_turn(*pend[0])]
+                pend = pend[1:]
+                pend.append((2 * pr, 0, h_step(pr, 0, [lambda: owed() and None], yq)))
+            else:
+                pend.append((2 * pr, 0, h_step(pr, 0, [], yq)))
+        with tc.manual_schedule():
+            for pr in range(PAIRS):
+                mid = []
+                if len(pend) >= YLAG:
+                    mid = [lambda item=pend[0]: y_turn(*item)]
+                    pend = pend[1:]
+                pend.append((2 * pr, 1, h_step(pr, 1, mid, last=(pr == PAIRS - 1))))
+            for item in pend:
+                y_turn(*item)()
+            store_scales()

@@ -19,10 +19,11 @@ PASSES = ITEMS // 512
 HALF = 512
 QUARTER = 256
 PAIRS = USERS // (2 * P)
-G_MULT = False
+G_MULT = True
 G_BOTH = False
-PRESORT = ()
-RING = 8
+FLAT_Z = False
+PRESORT = [("hist", v) for v in range(2, 8)]
+RING = 7
 SIDE_V_COLS = 256
 SIDE1_V_COLS = 192
 YLAG = 2
@@ -99,8 +100,9 @@ def tile_item_history_factors_h3_kernel(
         def presort(kind, r):
             if (kind, r) not in PRESORT:
                 return
-            s = keep.tile([P, ITEMS], BF16, name="sorted%d" % r, tag="rows%d" % (8 + len(presorted) % 4))
-            nc.scalar.copy(
+            s = keep.tile([P, ITEMS], BF16, name="sorted%d" % r, tag=("rows%d" % (8 + r % 4)) if kind == "hist" else "spare%d" % (r % 2))
+            copy = nc.vector.tensor_copy if kind == "sim" else nc.scalar.copy
+            copy(
                 out=s[:].bitcast(F32).rearrange("p (c u q) -> p c u q", c=PASSES, u=2),
                 in_=rows[kind, r][:].bitcast(F32).rearrange("p (c q u) -> p c u q", c=PASSES, u=2),
             )
@@ -174,6 +176,13 @@ def tile_item_history_factors_h3_kernel(
 
         def a_exit(bank, g, h, u, q, zpair):
             cols = slice(QUARTER * q, QUARTER * (q + 1))
+            if FLAT_Z:
+                nc.vector.scalar_tensor_tensor(
+                    out=zpair[:, u, :].rearrange("p (e n) -> p e n", e=2)[:, :, cols],
+                    in0=bank[:], scalar=0.0, in1=w_raw[g, h][:, 2 * u : 2 * u + 2, cols],
+                    op0=ALU.max, op1=ALU.mult,
+                )
+                return
             nc.vector.scalar_tensor_tensor(
                 out=zpair[:, u, 2 * QUARTER * q : 2 * QUARTER * (q + 1)].rearrange("p (n e) -> p n e", e=2),
                 in0=bank[:].rearrange("p e n -> p n e"),
@@ -194,6 +203,12 @@ def tile_item_history_factors_h3_kernel(
 
         def z_group(zpair):
             grouped = stage.tile([P, HALF * 4], BF16, name="grouped", bufs=3, align_bytes=64)
+            if FLAT_Z:
+                nc.scalar.copy(
+                    out=grouped[:].rearrange("p (c i t) -> p c t i", i=4, t=4),
+                    in_=zpair[:].rearrange("p u (e c i) -> p c (u e) i", e=2, i=4),
+                )
+                return grouped
             nc.scalar.copy(
                 out=grouped[:].bitcast(F32).rearrange("p (n u) -> p n u", u=2),
                 in_=zpair[:].bitcast(F32).rearrange("p u n -> p n u"),
@@ -314,7 +329,7 @@ def tile_item_history_factors_h3_kernel(
         def store_scales():
             scales_out = out_2.bitcast(I32)
             for quad in range(4):
-                nc.sync.dma_start(
+                (nc.scalar if quad % 2 == 0 else nc.sync).dma_start(
                     out=scales_out[:, 4 * quad : 4 * quad + 4, :].rearrange("g r m -> r g m"),
                     in_=y_scales[32 * quad : 32 * quad + 4, :, :].bitcast(I32),
                 )
@@ -327,10 +342,16 @@ def tile_item_history_factors_h3_kernel(
             codes, scales = moving["z", g, h]
             cols = slice(QUARTER * q, QUARTER * (q + 1))
             st = stage.tile([P, 2 * P * 4], BF16, name="turn_stage", bufs=5, align_bytes=64)
-            nc.scalar.copy(
-                out=st[:].bitcast(F32).rearrange("p (n u) -> p n u", u=2),
-                in_=zpair[:].bitcast(F32).rearrange("p u n -> p n u"),
-            )
+            if FLAT_Z:
+                nc.scalar.copy(
+                    out=st[:].rearrange("p (c i t) -> p c t i", i=4, t=4),
+                    in_=zpair[:].rearrange("p u (e c i) -> p c (u e) i", e=2, i=4),
+                )
+            else:
+                nc.scalar.copy(
+                    out=st[:].bitcast(F32).rearrange("p (n u) -> p n u", u=2),
+                    in_=zpair[:].bitcast(F32).rearrange("p u n -> p n u"),
+                )
             return lambda: nc.vector.quantize_mx(
                 out=codes[:, cols].bitcast(FP8X4), scales=scales[:, cols], in_=st[:]
             )
@@ -343,11 +364,12 @@ def tile_item_history_factors_h3_kernel(
                 for e in range(2):
                     for c in range(PASSES):
                         a_pass(bank, g, h, u, q, e, c)
+                order = "p e n -> p e n" if FLAT_Z else "p e n -> p n e"
                 nc.vector.scalar_tensor_tensor(
-                    out=zpair[:, u, :].rearrange("p (n e) -> p n e", e=2),
-                    in0=bank[:].rearrange("p e n -> p n e"),
+                    out=zpair[:, u, :].rearrange("p (e n) -> p e n" if FLAT_Z else "p (n e) -> p n e", e=2),
+                    in0=bank[:].rearrange(order),
                     scalar=0.0,
-                    in1=w_raw[g, h][:, 2 * u : 2 * u + 2, cols].rearrange("p e n -> p n e"),
+                    in1=w_raw[g, h][:, 2 * u : 2 * u + 2, cols].rearrange(order),
                     op0=ALU.max, op1=ALU.mult,
                 )
                 if u == 0:
@@ -376,7 +398,7 @@ def tile_item_history_factors_h3_kernel(
             if RING == 7:
                 gbank = psum.tile([P, D], BF16, name="gbank")
             else:
-                gbank = psum.tile([P, D], BF16, name="gbank", tag="bank7")
+                gbank = next_bank([P, D], BF16)
             for c in range(8):
                 nc.tensor.transpose(
                     gbank[:, P * c : P * (c + 1)], gain_cols[:, c : c + 1].to_broadcast([P, P]), ident16[:]
@@ -466,12 +488,16 @@ def tile_item_history_factors_h3_kernel(
         zp = new_zpair()
         for f in late:
             f()
+        presort("sim", 8)
+        presort("sim", 9)
         a_half(1, 0, 0, zp)
         zq()
         late = quants("sim", turn_run("sim", 8))
         sg0 = side_group(0, 1, SIDE1_V_COLS)
         late[0]()
         late[1]()
+        presort("sim", 10)
+        presort("sim", 11)
         a_half(1, 0, 1, zp, late[2:])
         late = quants("sim", turn_run("sim", 10))
         wide_quant("side", 0, 1, sg0)

@@ -19,11 +19,11 @@ PASSES = ITEMS // 512
 HALF = 512
 QUARTER = 256
 PAIRS = USERS // (2 * P)
-G_MULT = True
+G_MULT = False
 G_BOTH = False
 FLAT_Z = False
-PRESORT = [("hist", v) for v in range(2, 8)]
-RING = 7
+PRESORT = ()
+RING = 8
 SIDE_V_COLS = 256
 SIDE1_V_COLS = 192
 YLAG = 2
@@ -110,7 +110,7 @@ def tile_item_history_factors_h3_kernel(
             presorted.append((kind, r))
 
         def turn_bank(kind, a, j):
-            units = [(a, 0), (a, 1), (a, 2), (a + 1, 0), (a + 1, 1), (a + 1, 2)][2 * j : 2 * j + 2]
+            units = [(a + n // PASSES, n % PASSES) for n in (2 * j, 2 * j + 1)]
             bank = next_bank([P, 2, 2, P], F32)
             for s, (r, c) in enumerate(units):
                 words = rows[kind, r][:].bitcast(F32)
@@ -138,9 +138,9 @@ def tile_item_history_factors_h3_kernel(
             for s, (r, c) in enumerate(units):
                 turned[kind, r, c] = (codes[:, P * s : P * (s + 1)], scales[:, P * s : P * (s + 1)])
 
-        def turn_run(kind, a):
+        def turn_run(kind, a, js=(0, 1, 2)):
             staged = []
-            for j in range(3):
+            for j in js:
                 bank, units = turn_bank(kind, a, j)
                 staged.append((units, turn_exit(bank)))
             return staged
@@ -223,11 +223,16 @@ def tile_item_history_factors_h3_kernel(
                 f()
             a_bank(g, h, u, 1, zpair)
 
+        def run_all(calls):
+            for f in calls:
+                if f:
+                    f()
+
         def quant_later(kind, staged, j):
             return lambda: turn_quant(kind, staged[j][0], staged[j][1])
 
         def quants(kind, staged):
-            return [quant_later(kind, staged, j) for j in range(3)]
+            return [quant_later(kind, staged, j) for j in range(len(staged))]
 
         def zq_later(g, h, grouped):
             return lambda: wide_quant("z", g, h, grouped)
@@ -356,7 +361,7 @@ def tile_item_history_factors_h3_kernel(
                 out=codes[:, cols].bitcast(FP8X4), scales=scales[:, cols], in_=st[:]
             )
 
-        def a_quarter(g, h, q, between=()):
+        def a_quarter(g, h, q, between=(), after=None):
             zpair = stage.tile([P, 2, HALF], BF16, name="zquarter", bufs=2)
             cols = slice(QUARTER * q, QUARTER * (q + 1))
             for u in range(2):
@@ -373,9 +378,11 @@ def tile_item_history_factors_h3_kernel(
                     op0=ALU.max, op1=ALU.mult,
                 )
                 if u == 0:
-                    for f in between:
-                        f()
-            return z_quarter(g, h, q, zpair)
+                    owed = [f() for f in between]
+            made = z_quarter(g, h, q, zpair)
+            if after is not None:
+                after(owed)
+            return made
 
         def side_quarters(c):
             codes = keep.tile([P, HALF], U32, name="mc_side%d_0" % c, align_bytes=64)
@@ -445,11 +452,16 @@ def tile_item_history_factors_h3_kernel(
             first = {}
             for u, q in BANK_ORDER:
                 first[u, q] = next_bank([P, 2, QUARTER], F32)
+            def second_slot(u, q):
+                for c in range(PASSES):
+                    a_pass(first[u, q], 0, 0, u, q, 1, c)
+                a_exit(first[u, q], 0, 0, u, q, zp)
+
             owed = late[2]
             for c in range(PASSES):
                 sq = side_quarters(c)
                 owed()
-                if c > 0 and c < PASSES:
+                if c > 0:
                     for u in range(2):
                         a_pass(first[u, 1], 0, 0, u, 1, 0, c - 1)
                 sq[0]()
@@ -457,18 +469,20 @@ def tile_item_history_factors_h3_kernel(
                 if c == PASSES - 1:
                     owed()
                     nc.scalar.copy(out=gain[:], in_=gbank[:])
-                    late = quants("sim", turn_run("sim", 4))
+                    late = quants("sim", turn_run("sim", 4, (0, 1)))
                 for u in range(2):
                     a_pass(first[u, 0], 0, 0, u, 0, 0, c)
             for u in range(2):
                 a_pass(first[u, 1], 0, 0, u, 1, 0, PASSES - 1)
-            for f in late:
-                f()
-            for u, q in BANK_ORDER:
-                for c in range(PASSES):
-                    a_pass(first[u, q], 0, 0, u, q, 1, c)
-                a_exit(first[u, q], 0, 0, u, q, zp)
-        late = quants("sim", turn_run("sim", 6))
+            run_all(late)
+            second_slot(0, 0)
+            late = quants("sim", turn_run("sim", 4, (2, 3)))
+            second_slot(0, 1)
+            second_slot(1, 0)
+            run_all(late)
+            late = quants("sim", turn_run("sim", 4, (4, 5)))
+            second_slot(1, 1)
+            run_all(late)
 
         load_w(0, 1)
         load_base(0)
@@ -486,57 +500,40 @@ def tile_item_history_factors_h3_kernel(
 
         zq = zq_later(0, 0, z_group(zp))
         zp = new_zpair()
-        for f in late:
-            f()
-        presort("sim", 8)
-        presort("sim", 9)
-        a_half(1, 0, 0, zp)
-        zq()
-        late = quants("sim", turn_run("sim", 8))
-        sg0 = side_group(0, 1, SIDE1_V_COLS)
-        late[0]()
-        late[1]()
-        presort("sim", 10)
-        presort("sim", 11)
-        a_half(1, 0, 1, zp, late[2:])
-        late = quants("sim", turn_run("sim", 10))
-        wide_quant("side", 0, 1, sg0)
-        sg1 = side_group(1, 1, SIDE1_V_COLS)
+        late = [zq]
+        for i, (u, q) in enumerate(BANK_ORDER):
+            a_bank(1, 0, u, q, zp)
+            run_all(late)
+            if i < 3:
+                late = quants("sim", turn_run("sim", 8, (2 * i, 2 * i + 1)))
+                sg = side_group(i, 1, SIDE1_V_COLS)
+                late.append(lambda i=i, sg=sg: wide_quant("side", i, 1, sg))
         zq = zq_later(1, 0, z_group(zp))
         zp = new_zpair()
-        late[0]()
-        late[1]()
-        a_half(2, 0, 0, zp, late[2:])
-        sg2 = side_group(2, 1, SIDE1_V_COLS)
-        wide_quant("side", 1, 1, sg1)
+        a_half(2, 0, 0, zp)
         a_half(2, 0, 1, zp, [zq])
-        wide_quant("side", 2, 1, sg2)
 
         quarters = [(g, q) for g in range(PASSES) for q in range(2)]
         owed = zq_later(2, 0, z_group(zp))
         pend = []
         for pr in range(PAIRS):
-            late = quants("hist", turn_run("hist", 2 * pr))
-            yq = []
-            if pr >= 2:
-                yq = [y_turn(*pend[0])]
-                pend = pend[1:]
-            if pr < PAIRS - 1:
-                presort("hist", 2 * pr + 2)
-                presort("hist", 2 * pr + 3)
+            late = quants("hist", turn_run("hist", 2 * pr, (0, 1)))
             owed()
             late[0]()
-            owed = a_quarter(quarters[pr][0], 1, quarters[pr][1], late[1:])
+            mid = [lambda pr=pr: quants("hist", turn_run("hist", 2 * pr, (2,)))[0]]
+            if pr >= 2:
+                mid.append(lambda item=pend[0]: y_turn(*item))
+                pend = pend[1:]
+            mid.append(lambda f=late[1]: f())
+            owed = a_quarter(quarters[pr][0], 1, quarters[pr][1], mid, run_all)
             if pr == PAIRS - 1:
-                for f in yq:
-                    f()
                 nxt = a_quarter(2, 1, 0, [owed])
                 owed = a_quarter(2, 1, 1, [nxt])
                 yq = [y_turn(*pend[0])]
                 pend = pend[1:]
                 pend.append((2 * pr, 0, h_step(pr, 0, [lambda: owed() and None], yq)))
             else:
-                pend.append((2 * pr, 0, h_step(pr, 0, [], yq)))
+                pend.append((2 * pr, 0, h_step(pr, 0)))
         with tc.manual_schedule():
             for pr in range(PAIRS):
                 mid = []

@@ -21,11 +21,14 @@ QUARTER = 256
 PAIRS = USERS // (2 * P)
 G_MULT = False
 G_BOTH = False
-FLAT_Z = False
+FLAT_Z = True
+Z_V_COLS = 64
+ZQ_V_COLS = 0
+ZLAST_V_COLS = 128
 PRESORT = ()
 RING = 8
 SIDE_V_COLS = 256
-SIDE1_V_COLS = 192
+SIDE1_V_COLS = 256
 YLAG = 2
 
 
@@ -122,27 +125,35 @@ def tile_item_history_factors_h3_kernel(
                     nc.tensor.transpose(bank[:, s, u, :], src, ident32[:])
             return bank, units
 
-        def turn_exit(bank):
-            st = stage.tile([P, 2 * P * 4], BF16, name="turn_stage", bufs=5, align_bytes=64)
+        def turn_exit(bank, st):
             nc.scalar.copy(
-                out=st[:].bitcast(F32).rearrange("p (s m u) -> p s m u", s=2, u=2),
+                out=st.bitcast(F32).rearrange("p (s m u) -> p s m u", s=2, u=2),
                 in_=bank[:].rearrange("p s u m -> p s m u"),
             )
-            return st
 
         def turn_quant(kind, units, st):
             label = "%s%d_%d" % (kind, units[0][0], units[0][1])
-            codes = keep.tile([P, 2 * P], U32, name="tc_" + label, align_bytes=64)
-            scales = keep.tile([P, 2 * P], U8, name="ts_" + label, align_bytes=64)
+            codes = keep.tile([P, len(units) * P], U32, name="tc_" + label, align_bytes=64)
+            scales = keep.tile([P, len(units) * P], U8, name="ts_" + label, align_bytes=64)
             nc.vector.quantize_mx(out=codes[:].bitcast(FP8X4), scales=scales[:], in_=st[:])
             for s, (r, c) in enumerate(units):
                 turned[kind, r, c] = (codes[:, P * s : P * (s + 1)], scales[:, P * s : P * (s + 1)])
 
         def turn_run(kind, a, js=(0, 1, 2)):
             staged = []
+            if len(js) == 2:
+                st = stage.tile([P, HALF * 4], BF16, name="grouped", bufs=5, align_bytes=64)
+                both = []
+                for i, j in enumerate(js):
+                    bank, units = turn_bank(kind, a, j)
+                    turn_exit(bank, st[:, 1024 * i : 1024 * (i + 1)])
+                    both.extend(units)
+                return [(both, st)]
             for j in js:
                 bank, units = turn_bank(kind, a, j)
-                staged.append((units, turn_exit(bank)))
+                st = stage.tile([P, 2 * P * 4], BF16, name="turn_stage", bufs=4, align_bytes=64)
+                turn_exit(bank, st[:])
+                staged.append((units, st))
             return staged
 
         moving = {}
@@ -154,7 +165,7 @@ def tile_item_history_factors_h3_kernel(
             moving[kind, c, h] = (codes, scales)
 
         def side_group(c, h, v_cols):
-            grouped = stage.tile([P, HALF * 4], BF16, name="grouped", bufs=3, align_bytes=64)
+            grouped = stage.tile([P, HALF * 4], BF16, name="grouped", bufs=5, align_bytes=64)
             dst = grouped[:].rearrange("p (c i t) -> p c t i", i=4, t=4)
             src = side_raw[c, h][:].rearrange("p t (c i) -> p c t i", i=4)
             cut = v_cols // 4
@@ -202,12 +213,14 @@ def tile_item_history_factors_h3_kernel(
             a_exit(bank, g, h, u, q, zpair)
 
         def z_group(zpair):
-            grouped = stage.tile([P, HALF * 4], BF16, name="grouped", bufs=3, align_bytes=64)
+            grouped = stage.tile([P, HALF * 4], BF16, name="grouped", bufs=5, align_bytes=64)
             if FLAT_Z:
-                nc.scalar.copy(
-                    out=grouped[:].rearrange("p (c i t) -> p c t i", i=4, t=4),
-                    in_=zpair[:].rearrange("p u (e c i) -> p c (u e) i", e=2, i=4),
-                )
+                dst = grouped[:].rearrange("p (c i t) -> p c t i", i=4, t=4)
+                src = zpair[:].rearrange("p u (e c i) -> p c (u e) i", e=2, i=4)
+                cut = Z_V_COLS // 4
+                if cut:
+                    nc.vector.tensor_copy(out=dst[:, :cut], in_=src[:, :cut])
+                nc.scalar.copy(out=dst[:, cut:], in_=src[:, cut:])
                 return grouped
             nc.scalar.copy(
                 out=grouped[:].bitcast(F32).rearrange("p (n u) -> p n u", u=2),
@@ -281,7 +294,7 @@ def tile_item_history_factors_h3_kernel(
             dst = out_0[2 * P * pr : 2 * P * (pr + 1), cols].rearrange("(v p) d -> p v d", p=P)
             ysorts = []
             for v in range(2):
-                ysorts.append(stage.tile([P, HALF], BF16, name="ysort", bufs=8))
+                ysorts.append(stage.tile([P, HALF], BF16, name="ysort", bufs=6))
             s0 = h_bank(2 * pr, h)
             first_on_gpsimd = G_MULT and not (last and G_BOTH)
             if first_on_gpsimd:
@@ -293,12 +306,7 @@ def tile_item_history_factors_h3_kernel(
             if last:
                 y_round(y[:, 0, :], ysorts[0][:])
                 nc.sync.dma_start(out=dst[:, 0, :], in_=y[:, 0, :])
-                nc.vector.tensor_tensor(
-                    out=ysorts[1][:].rearrange("p (u q e) -> p u q e", u=2, e=2),
-                    in0=s1[:].rearrange("p (q u e) -> p u q e", u=2, e=2),
-                    in1=gain_src[0][:, cols].rearrange("p (q u e) -> p u q e", u=2, e=2),
-                    op=ALU.mult,
-                )
+                y_mult(h, s1, ysorts[1][:], False)
                 ylast = stage.tile([P, 2, HALF], F32, name="y", bufs=4)
                 y_mult(h, s1, ylast[:, 1, :], False)
                 nc.sync.dma_start(out=dst[:, 1, :], in_=ylast[:, 1, :])
@@ -317,8 +325,9 @@ def tile_item_history_factors_h3_kernel(
             for s in range(n):
                 words = ysorts[s][:].bitcast(F32)
                 for u in range(2):
-                    nc.tensor.transpose(bank[:, s, u, :], words[:, P * u : P * (u + 1)], ident32[:])
-            st = stage.tile([P, n * P * 4], BF16, name="turn_stage", bufs=5, align_bytes=64)
+                    src = words[:, u::2] if (first_tile + s, h) == (7, 1) else words[:, P * u : P * (u + 1)]
+                    nc.tensor.transpose(bank[:, s, u, :], src, ident32[:])
+            st = stage.tile([P, n * P * 4], BF16, name="turn_stage", bufs=4, align_bytes=64)
             nc.scalar.copy(
                 out=st[:].bitcast(F32).rearrange("p (s m u) -> p s m u", s=n, u=2),
                 in_=bank[:].rearrange("p s u m -> p s m u"),
@@ -346,12 +355,14 @@ def tile_item_history_factors_h3_kernel(
                 moving["z", g, h] = (codes, scales)
             codes, scales = moving["z", g, h]
             cols = slice(QUARTER * q, QUARTER * (q + 1))
-            st = stage.tile([P, 2 * P * 4], BF16, name="turn_stage", bufs=5, align_bytes=64)
+            st = stage.tile([P, 2 * P * 4], BF16, name="turn_stage", bufs=4, align_bytes=64)
             if FLAT_Z:
-                nc.scalar.copy(
-                    out=st[:].rearrange("p (c i t) -> p c t i", i=4, t=4),
-                    in_=zpair[:].rearrange("p u (e c i) -> p c (u e) i", e=2, i=4),
-                )
+                dst = st[:].rearrange("p (c i t) -> p c t i", i=4, t=4)
+                src = zpair[:].rearrange("p u (e c i) -> p c (u e) i", e=2, i=4)
+                cut = (ZLAST_V_COLS if (g, q) == (2, 1) else ZQ_V_COLS) // 4
+                if cut:
+                    nc.vector.tensor_copy(out=dst[:, :cut], in_=src[:, :cut])
+                nc.scalar.copy(out=dst[:, cut:], in_=src[:, cut:])
             else:
                 nc.scalar.copy(
                     out=st[:].bitcast(F32).rearrange("p (n u) -> p n u", u=2),
@@ -362,7 +373,7 @@ def tile_item_history_factors_h3_kernel(
             )
 
         def a_quarter(g, h, q, between=(), after=None):
-            zpair = stage.tile([P, 2, HALF], BF16, name="zquarter", bufs=2)
+            zpair = stage.tile([P, 2, HALF], BF16, name="zquarter", tag="zpair", bufs=2)
             cols = slice(QUARTER * q, QUARTER * (q + 1))
             for u in range(2):
                 bank = next_bank([P, 2, QUARTER], F32)
@@ -391,7 +402,7 @@ def tile_item_history_factors_h3_kernel(
             src = side_raw[c, 0][:].rearrange("p t (c i) -> p c t i", i=4)
             calls = []
             for q, copy in enumerate((nc.vector.tensor_copy, nc.scalar.copy)):
-                st = stage.tile([P, 2 * P * 4], BF16, name="turn_stage", bufs=5, align_bytes=64)
+                st = stage.tile([P, 2 * P * 4], BF16, name="turn_stage", bufs=4, align_bytes=64)
                 copy(out=st[:].rearrange("p (c i t) -> p c t i", i=4, t=4), in_=src[:, 64 * q : 64 * (q + 1)])
                 cols = slice(QUARTER * q, QUARTER * (q + 1))
                 calls.append(
@@ -488,10 +499,10 @@ def tile_item_history_factors_h3_kernel(
         load_base(0)
         load_hist(2)
         load_hist(3)
+        load_w(1, 1)
         load_base(1)
         load_hist(4)
         load_hist(5)
-        load_w(1, 1)
         load_base(2)
         load_hist(6)
         load_hist(7)
@@ -511,24 +522,27 @@ def tile_item_history_factors_h3_kernel(
         zq = zq_later(1, 0, z_group(zp))
         zp = new_zpair()
         a_half(2, 0, 0, zp)
+        late = quants("hist", turn_run("hist", 0, (0, 1)))
         a_half(2, 0, 1, zp, [zq])
 
         quarters = [(g, q) for g in range(PASSES) for q in range(2)]
         owed = zq_later(2, 0, z_group(zp))
         pend = []
         for pr in range(PAIRS):
-            late = quants("hist", turn_run("hist", 2 * pr, (0, 1)))
+            if pr > 0:
+                late = quants("hist", turn_run("hist", 2 * pr, (0, 1)))
             owed()
-            late[0]()
             mid = [lambda pr=pr: quants("hist", turn_run("hist", 2 * pr, (2,)))[0]]
             if pr >= 2:
                 mid.append(lambda item=pend[0]: y_turn(*item))
                 pend = pend[1:]
-            mid.append(lambda f=late[1]: f())
-            owed = a_quarter(quarters[pr][0], 1, quarters[pr][1], mid, run_all)
+            mid.append(lambda f=late[0]: f())
+            g, q = quarters[pr + 1 if pr > 0 else 0]
+            owed = a_quarter(g, 1, q, mid, run_all)
+            if pr == 0:
+                owed = a_quarter(0, 1, 1, [owed])
             if pr == PAIRS - 1:
-                nxt = a_quarter(2, 1, 0, [owed])
-                owed = a_quarter(2, 1, 1, [nxt])
+                owed = a_quarter(2, 1, 1, [owed])
                 yq = [y_turn(*pend[0])]
                 pend = pend[1:]
                 pend.append((2 * pr, 0, h_step(pr, 0, [lambda: owed() and None], yq)))

@@ -22,13 +22,14 @@ PAIRS = USERS // (2 * P)
 G_MULT = False
 G_BOTH = False
 FLAT_Z = True
+FLAT0 = False
 Z_V_COLS = 64
 ZQ_V_COLS = 0
 ZLAST_V_COLS = 128
 PRESORT = ()
 RING = 8
 SIDE_V_COLS = 256
-SIDE1_V_COLS = 256
+SIDE1_V_COLS = 128
 YLAG = 2
 
 
@@ -187,7 +188,7 @@ def tile_item_history_factors_h3_kernel(
 
         def a_exit(bank, g, h, u, q, zpair):
             cols = slice(QUARTER * q, QUARTER * (q + 1))
-            if FLAT_Z:
+            if FLAT0:
                 nc.vector.scalar_tensor_tensor(
                     out=zpair[:, u, :].rearrange("p (e n) -> p e n", e=2)[:, :, cols],
                     in0=bank[:], scalar=0.0, in1=w_raw[g, h][:, 2 * u : 2 * u + 2, cols],
@@ -214,7 +215,7 @@ def tile_item_history_factors_h3_kernel(
 
         def z_group(zpair):
             grouped = stage.tile([P, HALF * 4], BF16, name="grouped", bufs=5, align_bytes=64)
-            if FLAT_Z:
+            if FLAT0:
                 dst = grouped[:].rearrange("p (c i t) -> p c t i", i=4, t=4)
                 src = zpair[:].rearrange("p u (e c i) -> p c (u e) i", e=2, i=4)
                 cut = Z_V_COLS // 4

from contextlib import ExitStack

import concourse.mybir as mybir
from concourse.masks import make_identity

ITEMS, D, USERS = 1536, 1024, 1024
FLOPS = 2 * ITEMS * ITEMS * D + 2 * USERS * ITEMS * D

F32 = mybir.dt.float32
BF16 = mybir.dt.bfloat16
U32 = mybir.dt.uint32
I32 = mybir.dt.int32
U8 = mybir.dt.uint8
FP8X4 = mybir.dt.float8_e4m3fn_x4
ALU = mybir.AluOpType

P = 128
PASSES = ITEMS // 512
HALF = 512
QUARTER = 256
PAIRS = USERS // (2 * P)
G_MULT = False
G_BOTH = False
FLAT_Z = True
FLAT0 = False
Z_V_COLS = 64
ZQ_V_COLS = 0
ZLAST_V_COLS = 128
PRESORT = ()
RING = 8
SIDE_V_COLS = 256
SIDE1_V_COLS = 128
YLAG = 2


def tile_item_history_factors_h3_kernel(
    tc, sim, side, factor_w, history, user_base, user_scale, factor_gain, out_0, out_1, out_2
):
    nc = tc.nc
    with ExitStack() as ctx:
        keep = ctx.enter_context(tc.tile_pool(name="keep", bufs=1))
        stage = ctx.enter_context(tc.tile_pool(name="stage", bufs=1))
        psum = ctx.enter_context(tc.psum_pool(name="psum", bufs=1))
        ctx.enter_context(tc.manual_schedule(engines={mybir.EngineType.PE, mybir.EngineType.SP}))

        banks_taken = []

        def next_bank(shape, dtype):
            n = len(banks_taken)
            banks_taken.append(n)
            return psum.tile(shape, dtype, name="bank%d" % n, tag="bank%d" % (n % RING))

        ident32 = keep.tile([P, P], F32, name="ident32")
        ident16 = keep.tile([P, P], BF16, name="ident16")
        vec_rows = keep.tile([P, P], BF16, name="vec_rows")
        nc.gpsimd.memset(vec_rows[:], 0.0)
        make_identity(nc, ident32[:])
        make_identity(nc, ident16[:])

        rows = {}
        side_raw = {}
        w_raw = {}
        base_raw = {}

        def load_sim(g, t):
            r = keep.tile([P, ITEMS], BF16, name="sim%d_%d" % (g, t), tag="rows%d" % (4 * g + t))
            nc.sync.dma_start(
                out=r[:], in_=sim[512 * g : 512 * (g + 1), :].rearrange("(m t) k -> m t k", t=4)[:, t, :]
            )
            rows["sim", 4 * g + t] = r

        def load_hist(v):
            r = keep.tile([P, ITEMS], BF16, name="hist%d" % v, tag="rows%d" % v)
            nc.sync.dma_start(out=r[:], in_=history[P * v : P * (v + 1), :])
            rows["hist", v] = r

        def load_k_first(src, store, label, g, h):
            slot = ("side", g, 0) if (label, h) == ("w", 1) else (label, g, h)
            r = keep.tile([P, 4, HALF], BF16, name="%s%d_%d" % (label, g, h), tag="%s%d_%d" % slot)
            nc.sync.dma_start(
                out=r[:],
                in_=src[512 * g : 512 * (g + 1), HALF * h : HALF * (h + 1)].rearrange("(p j) n -> p j n", j=4),
            )
            store[g, h] = r

        def load_side(h):
            for c in range(PASSES):
                load_k_first(side, side_raw, "side", c, h)

        def load_w(g, h):
            load_k_first(factor_w, w_raw, "w", g, h)

        def load_base(pr):
            r = keep.tile([P, 2, D], BF16, name="base%d" % pr)
            nc.sync.dma_start(
                out=r[:], in_=user_base[2 * P * pr : 2 * P * (pr + 1), :].rearrange("(v p) d -> p v d", p=P)
            )
            base_raw[pr] = r

        turned = {}

        presorted = []

        def presort(kind, r):
            if (kind, r) not in PRESORT:
                return
            s = keep.tile([P, ITEMS], BF16, name="sorted%d" % r, tag=("rows%d" % (8 + r % 4)) if kind == "hist" else "spare%d" % (r % 2))
            copy = nc.vector.tensor_copy if kind == "sim" else nc.scalar.copy
            copy(
                out=s[:].bitcast(F32).rearrange("p (c u q) -> p c u q", c=PASSES, u=2),
                in_=rows[kind, r][:].bitcast(F32).rearrange("p (c q u) -> p c u q", c=PASSES, u=2),
            )
            rows[kind, r] = s
            presorted.append((kind, r))

        def turn_bank(kind, a, j):
            units = [(a + n // PASSES, n % PASSES) for n in (2 * j, 2 * j + 1)]
            bank = next_bank([P, 2, 2, P], F32)
            for s, (r, c) in enumerate(units):
                words = rows[kind, r][:].bitcast(F32)
                for u in range(2):
                    if (kind, r) in presorted:
                        src = words[:, 256 * c + P * u : 256 * c + P * (u + 1)]
                    else:
                        src = words[:, 256 * c + u : 256 * (c + 1) : 2]
                    nc.tensor.transpose(bank[:, s, u, :], src, ident32[:])
            return bank, units

        def turn_exit(bank, st):
            nc.scalar.copy(
                out=st.bitcast(F32).rearrange("p (s m u) -> p s m u", s=2, u=2),
                in_=bank[:].rearrange("p s u m -> p s m u"),
            )

        def turn_quant(kind, units, st):
            label = "%s%d_%d" % (kind, units[0][0], units[0][1])
            codes = keep.tile([P, len(units) * P], U32, name="tc_" + label, align_bytes=64)
            scales = keep.tile([P, len(units) * P], U8, name="ts_" + label, align_bytes=64)
            nc.vector.quantize_mx(out=codes[:].bitcast(FP8X4), scales=scales[:], in_=st[:])
            for s, (r, c) in enumerate(units):
                turned[kind, r, c] = (codes[:, P * s : P * (s + 1)], scales[:, P * s : P * (s + 1)])

        def turn_run(kind, a, js=(0, 1, 2)):
            staged = []
            if len(js) == 2:
                st = stage.tile([P, HALF * 4], BF16, name="grouped", bufs=5, align_bytes=64)
                both = []
                for i, j in enumerate(js):
                    bank, units = turn_bank(kind, a, j)
                    turn_exit(bank, st[:, 1024 * i : 1024 * (i + 1)])
                    both.extend(units)
                return [(both, st)]
            for j in js:
                bank, units = turn_bank(kind, a, j)
                st = stage.tile([P, 2 * P * 4], BF16, name="turn_stage", bufs=4, align_bytes=64)
                turn_exit(bank, st[:])
                staged.append((units, st))
            return staged

        moving = {}

        def wide_quant(kind, c, h, grouped):
            codes = keep.tile([P, HALF], U32, name="mc_%s%d_%d" % (kind, c, h), align_bytes=64)
            scales = keep.tile([P, HALF], U8, name="ms_%s%d_%d" % (kind, c, h), align_bytes=64)
            nc.vector.quantize_mx(out=codes[:].bitcast(FP8X4), scales=scales[:], in_=grouped[:])
            moving[kind, c, h] = (codes, scales)

        def side_group(c, h, v_cols):
            grouped = stage.tile([P, HALF * 4], BF16, name="grouped", bufs=5, align_bytes=64)
            dst = grouped[:].rearrange("p (c i t) -> p c t i", i=4, t=4)
            src = side_raw[c, h][:].rearrange("p t (c i) -> p c t i", i=4)
            cut = v_cols // 4
            if cut > 0:
                nc.vector.tensor_copy(out=dst[:, :cut], in_=src[:, :cut])
            if cut < HALF // 4:
                nc.scalar.copy(out=dst[:, cut:], in_=src[:, cut:])
            return grouped

        def a_pass(bank, g, h, u, q, e, c):
            lc, ls = turned["sim", 4 * g + 2 * u + e, c]
            rc, rs = moving["side", c, h]
            cols = slice(QUARTER * q, QUARTER * (q + 1))
            nc.tensor.matmul_mx(
                out=bank[:, e, :], lhsT=lc.bitcast(FP8X4), lhsT_scale=ls,
                rhs=rc[:, cols].bitcast(FP8X4), rhs_scale=rs[:, cols],
                start=(c == 0), stop=(c == PASSES - 1),
            )

        def a_exit(bank, g, h, u, q, zpair):
            cols = slice(QUARTER * q, QUARTER * (q + 1))
            if FLAT0:
                nc.vector.scalar_tensor_tensor(
                    out=zpair[:, u, :].rearrange("p (e n) -> p e n", e=2)[:, :, cols],
                    in0=bank[:], scalar=0.0, in1=w_raw[g, h][:, 2 * u : 2 * u + 2, cols],
                    op0=ALU.max, op1=ALU.mult,
                )
                return
            nc.vector.scalar_tensor_tensor(
                out=zpair[:, u, 2 * QUARTER * q : 2 * QUARTER * (q + 1)].rearrange("p (n e) -> p n e", e=2),
                in0=bank[:].rearrange("p e n -> p n e"),
                scalar=0.0,
                in1=w_raw[g, h][:, 2 * u : 2 * u + 2, cols].rearrange("p e n -> p n e"),
                op0=ALU.max, op1=ALU.mult,
            )

        def new_zpair():
            return stage.tile([P, 2, 2 * HALF], BF16, name="zpair", bufs=2)

        def a_bank(g, h, u, q, zpair):
            bank = next_bank([P, 2, QUARTER], F32)
            for e in range(2):
                for c in range(PASSES):
                    a_pass(bank, g, h, u, q, e, c)
            a_exit(bank, g, h, u, q, zpair)

        def z_group(zpair):
            grouped = stage.tile([P, HALF * 4], BF16, name="grouped", bufs=5, align_bytes=64)
            if FLAT0:
                dst = grouped[:].rearrange("p (c i t) -> p c t i", i=4, t=4)
                src = zpair[:].rearrange("p u (e c i) -> p c (u e) i", e=2, i=4)
                cut = Z_V_COLS // 4
                if cut:
                    nc.vector.tensor_copy(out=dst[:, :cut], in_=src[:, :cut])
                nc.scalar.copy(out=dst[:, cut:], in_=src[:, cut:])
                return grouped
            nc.scalar.copy(
                out=grouped[:].bitcast(F32).rearrange("p (n u) -> p n u", u=2),
                in_=zpair[:].bitcast(F32).rearrange("p u n -> p n u"),
            )
            return grouped

        BANK_ORDER = [(0, 0), (0, 1), (1, 0), (1, 1)]

        def a_half(g, h, u, zpair, between=()):
            a_bank(g, h, u, 0, zpair)
            for f in between:
                f()
            a_bank(g, h, u, 1, zpair)

        def run_all(calls):
            for f in calls:
                if f:
                    f()

        def quant_later(kind, staged, j):
            return lambda: turn_quant(kind, staged[j][0], staged[j][1])

        def quants(kind, staged):
            return [quant_later(kind, staged, j) for j in range(len(staged))]

        def zq_later(g, h, grouped):
            return lambda: wide_quant("z", g, h, grouped)

        y_scales = keep.tile([P, 2, USERS], U8, name="y_scales", align_bytes=64)
        words_out = out_1.rearrange("g p m t -> g p (m t)").bitcast(I32)
        gain_cols = keep.tile([P, 8], BF16, name="gain_cols")
        scale_cols = keep.tile([P, 8], F32, name="scale_cols")
        gain = keep.tile([P, D], BF16, name="gain")

        gain_src = []

        def h_bank(v, h):
            bank = next_bank([P, HALF], F32)
            for c in range(PASSES):
                lc, ls = turned["hist", v, c]
                rc, rs = moving["z", c, h]
                nc.tensor.matmul_mx(
                    out=bank[:], lhsT=lc.bitcast(FP8X4), lhsT_scale=ls,
                    rhs=rc[:].bitcast(FP8X4), rhs_scale=rs[:],
                    start=(c == 0), stop=(c == PASSES - 1),
                )
            s = stage.tile([P, HALF], F32, name="sums", bufs=4)
            nc.vector.scalar_tensor_tensor(
                out=s[:], in0=bank[:], scalar=scale_cols[:, v : v + 1],
                in1=base_raw[v // 2][:, v % 2, HALF * h : HALF * (h + 1)], op0=ALU.mult, op1=ALU.add,
            )
            return s

        def y_mult(h, s, y, on_gpsimd):
            cols = slice(HALF * h, HALF * (h + 1))
            if on_gpsimd:
                nc.gpsimd.tensor_tensor(out=y, in0=s[:], in1=gain[:, cols], op=ALU.mult)
            else:
                nc.vector.tensor_tensor(out=y, in0=s[:], in1=gain_src[0][:, cols], op=ALU.mult)

        def y_round(y, ysort):
            nc.scalar.copy(
                out=ysort.rearrange("p (u q e) -> p u q e", u=2, e=2),
                in_=y.rearrange("p (q u e) -> p u q e", u=2, e=2),
            )

        def h_step(pr, h, mid=(), between=(), last=False):
            cols = slice(HALF * h, HALF * (h + 1))
            y = stage.tile([P, 2, HALF], F32, name="y", bufs=4)
            dst = out_0[2 * P * pr : 2 * P * (pr + 1), cols].rearrange("(v p) d -> p v d", p=P)
            ysorts = []
            for v in range(2):
                ysorts.append(stage.tile([P, HALF], BF16, name="ysort", bufs=6))
            s0 = h_bank(2 * pr, h)
            first_on_gpsimd = G_MULT and not (last and G_BOTH)
            if first_on_gpsimd:
                y_mult(h, s0, y[:, 0, :], True)
            owed = [f() for f in mid]
            s1 = h_bank(2 * pr + 1, h)
            if not first_on_gpsimd:
                y_mult(h, s0, y[:, 0, :], False)
            if last:
                y_round(y[:, 0, :], ysorts[0][:])
                nc.sync.dma_start(out=dst[:, 0, :], in_=y[:, 0, :])
                y_mult(h, s1, ysorts[1][:], False)
                ylast = stage.tile([P, 2, HALF], F32, name="y", bufs=4)
                y_mult(h, s1, ylast[:, 1, :], False)
                nc.sync.dma_start(out=dst[:, 1, :], in_=ylast[:, 1, :])
            else:
                y_mult(h, s1, y[:, 1, :], G_BOTH)
                for v in range(2):
                    y_round(y[:, v, :], ysorts[v][:])
                nc.sync.dma_start(out=dst, in_=y[:])
            for f in list(between) + [f for f in owed if f]:
                f()
            return ysorts

        def y_turn(first_tile, h, ysorts):
            n = len(ysorts)
            bank = next_bank([P, n, 2, P], F32)
            for s in range(n):
                words = ysorts[s][:].bitcast(F32)
                for u in range(2):
                    src = words[:, u::2] if (first_tile + s, h) == (7, 1) else words[:, P * u : P * (u + 1)]
                    nc.tensor.transpose(bank[:, s, u, :], src, ident32[:])
            st = stage.tile([P, n * P * 4], BF16, name="turn_stage", bufs=4, align_bytes=64)
            nc.scalar.copy(
                out=st[:].bitcast(F32).rearrange("p (s m u) -> p s m u", s=n, u=2),
                in_=bank[:].rearrange("p s u m -> p s m u"),
            )
            return lambda: y_quant(first_tile, n, h, st)

        def y_quant(first_tile, n, h, st):
            users = slice(P * first_tile, P * (first_tile + n))
            codes = stage.tile([P, n * P], U32, name="y_codes", bufs=5, align_bytes=64)
            nc.vector.quantize_mx(out=codes[:].bitcast(FP8X4), scales=y_scales[:, h, users], in_=st[:])
            nc.sync.dma_start(out=words_out[h, :, users], in_=codes[:].bitcast(I32))

        def store_scales():
            scales_out = out_2.bitcast(I32)
            for quad in range(4):
                (nc.scalar if quad % 2 == 0 else nc.sync).dma_start(
                    out=scales_out[:, 4 * quad : 4 * quad + 4, :].rearrange("g r m -> r g m"),
                    in_=y_scales[32 * quad : 32 * quad + 4, :, :].bitcast(I32),
                )

        def z_quarter(g, h, q, zpair):
            if q == 0:
                codes = keep.tile([P, HALF], U32, name="mc_z%d_%d" % (g, h), align_bytes=64)
                scales = keep.tile([P, HALF], U8, name="ms_z%d_%d" % (g, h), align_bytes=64)
                moving["z", g, h] = (codes, scales)
            codes, scales = moving["z", g, h]
            cols = slice(QUARTER * q, QUARTER * (q + 1))
            st = stage.tile([P, 2 * P * 4], BF16, name="turn_stage", bufs=4, align_bytes=64)
            if FLAT_Z:
                dst = st[:].rearrange("p (c i t) -> p c t i", i=4, t=4)
                src = zpair[:].rearrange("p u (e c i) -> p c (u e) i", e=2, i=4)
                cut = (ZLAST_V_COLS if (g, q) == (2, 1) else ZQ_V_COLS) // 4
                if cut:
                    nc.vector.tensor_copy(out=dst[:, :cut], in_=src[:, :cut])
                nc.scalar.copy(out=dst[:, cut:], in_=src[:, cut:])
            else:
                nc.scalar.copy(
                    out=st[:].bitcast(F32).rearrange("p (n u) -> p n u", u=2),
                    in_=zpair[:].bitcast(F32).rearrange("p u n -> p n u"),
                )
            return lambda: nc.vector.quantize_mx(
                out=codes[:, cols].bitcast(FP8X4), scales=scales[:, cols], in_=st[:]
            )

        def a_quarter(g, h, q, between=(), after=None):
            zpair = stage.tile([P, 2, HALF], BF16, name="zquarter", tag="zpair", bufs=2)
            cols = slice(QUARTER * q, QUARTER * (q + 1))
            for u in range(2):
                bank = next_bank([P, 2, QUARTER], F32)
                for e in range(2):
                    for c in range(PASSES):
                        a_pass(bank, g, h, u, q, e, c)
                order = "p e n -> p e n" if FLAT_Z else "p e n -> p n e"
                nc.vector.scalar_tensor_tensor(
                    out=zpair[:, u, :].rearrange("p (e n) -> p e n" if FLAT_Z else "p (n e) -> p n e", e=2),
                    in0=bank[:].rearrange(order),
                    scalar=0.0,
                    in1=w_raw[g, h][:, 2 * u : 2 * u + 2, cols].rearrange(order),
                    op0=ALU.max, op1=ALU.mult,
                )
                if u == 0:
                    owed = [f() for f in between]
            made = z_quarter(g, h, q, zpair)
            if after is not None:
                after(owed)
            return made

        def side_quarters(c):
            codes = keep.tile([P, HALF], U32, name="mc_side%d_0" % c, align_bytes=64)
            scales = keep.tile([P, HALF], U8, name="ms_side%d_0" % c, align_bytes=64)
            moving["side", c, 0] = (codes, scales)
            src = side_raw[c, 0][:].rearrange("p t (c i) -> p c t i", i=4)
            calls = []
            for q, copy in enumerate((nc.vector.tensor_copy, nc.scalar.copy)):
                st = stage.tile([P, 2 * P * 4], BF16, name="turn_stage", bufs=4, align_bytes=64)
                copy(out=st[:].rearrange("p (c i t) -> p c t i", i=4, t=4), in_=src[:, 64 * q : 64 * (q + 1)])
                cols = slice(QUARTER * q, QUARTER * (q + 1))
                calls.append(
                    lambda cols=cols, st=st: nc.vector.quantize_mx(
                        out=codes[:, cols].bitcast(FP8X4), scales=scales[:, cols], in_=st[:]
                    )
                )
            return calls

        def make_gain():
            if RING == 7:
                gbank = psum.tile([P, D], BF16, name="gbank")
            else:
                gbank = next_bank([P, D], BF16)
            for c in range(8):
                nc.tensor.transpose(
                    gbank[:, P * c : P * (c + 1)], gain_cols[:, c : c + 1].to_broadcast([P, P]), ident16[:]
                )
            gain_src.append(gbank if RING == 7 else gain)
            return gbank

        for t in range(4):
            load_sim(0, t)
        nc.sync.dma_start(out=vec_rows[0:8, :], in_=factor_gain.rearrange("(c p) -> c p", p=P))
        nc.sync.dma_start(out=vec_rows[8:16, :], in_=user_scale.rearrange("(c p) -> c p", p=P))
        load_side(0)
        load_sim(1, 0)
        load_sim(1, 1)
        load_w(0, 0)
        load_sim(1, 2)
        load_sim(1, 3)
        load_w(1, 0)
        load_sim(2, 0)
        load_sim(2, 1)
        load_k_first(side, side_raw, "side", 0, 1)
        load_sim(2, 2)
        load_sim(2, 3)
        load_k_first(side, side_raw, "side", 1, 1)
        load_w(2, 0)
        load_k_first(side, side_raw, "side", 2, 1)

        with tc.manual_schedule():
            for f in quants("sim", turn_run("sim", 0)):
                f()
            late = quants("sim", turn_run("sim", 2))
            vbank = next_bank([P, P], BF16)
            nc.tensor.transpose(vbank[:], vec_rows[:], ident16[:])
            late[0]()
            nc.vector.tensor_copy(out=gain_cols[:], in_=vbank[:, 0:8])
            nc.vector.tensor_copy(out=scale_cols[:], in_=vbank[:, 8:16])
            late[1]()
            gbank = make_gain()

            load_hist(0)
            load_hist(1)

            zp = new_zpair()
            first = {}
            for u, q in BANK_ORDER:
                first[u, q] = next_bank([P, 2, QUARTER], F32)
            def second_slot(u, q):
                for c in range(PASSES):
                    a_pass(first[u, q], 0, 0, u, q, 1, c)
                a_exit(first[u, q], 0, 0, u, q, zp)

            owed = late[2]
            for c in range(PASSES):
                sq = side_quarters(c)
                owed()
                if c > 0:
                    for u in range(2):
                        a_pass(first[u, 1], 0, 0, u, 1, 0, c - 1)
                sq[0]()
                owed = sq[1]
                if c == PASSES - 1:
                    owed()
                    nc.scalar.copy(out=gain[:], in_=gbank[:])
                    late = quants("sim", turn_run("sim", 4, (0, 1)))
                for u in range(2):
                    a_pass(first[u, 0], 0, 0, u, 0, 0, c)
            for u in range(2):
                a_pass(first[u, 1], 0, 0, u, 1, 0, PASSES - 1)
            run_all(late)
            second_slot(0, 0)
            late = quants("sim", turn_run("sim", 4, (2, 3)))
            second_slot(0, 1)
            second_slot(1, 0)
            run_all(late)
            late = quants("sim", turn_run("sim", 4, (4, 5)))
            second_slot(1, 1)
            run_all(late)

        load_w(0, 1)
        load_base(0)
        load_hist(2)
        load_hist(3)
        load_w(1, 1)
        load_base(1)
        load_hist(4)
        load_hist(5)
        load_base(2)
        load_hist(6)
        load_hist(7)
        load_w(2, 1)
        load_base(3)

        zq = zq_later(0, 0, z_group(zp))
        zp = new_zpair()
        late = [zq]
        for i, (u, q) in enumerate(BANK_ORDER):
            a_bank(1, 0, u, q, zp)
            run_all(late)
            if i < 3:
                late = quants("sim", turn_run("sim", 8, (2 * i, 2 * i + 1)))
                sg = side_group(i, 1, SIDE1_V_COLS)
                late.append(lambda i=i, sg=sg: wide_quant("side", i, 1, sg))
        zq = zq_later(1, 0, z_group(zp))
        zp = new_zpair()
        a_half(2, 0, 0, zp)
        late = quants("hist", turn_run("hist", 0, (0, 1)))
        a_half(2, 0, 1, zp, [zq])

        quarters = [(g, q) for g in range(PASSES) for q in range(2)]
        owed = zq_later(2, 0, z_group(zp))
        pend = []
        for pr in range(PAIRS):
            if pr > 0:
                late = quants("hist", turn_run("hist", 2 * pr, (0, 1)))
            owed()
            mid = [lambda pr=pr: quants("hist", turn_run("hist", 2 * pr, (2,)))[0]]
            if pr >= 2:
                mid.append(lambda item=pend[0]: y_turn(*item))
                pend = pend[1:]
            mid.append(lambda f=late[0]: f())
            g, q = quarters[pr + 1 if pr > 0 else 0]
            owed = a_quarter(g, 1, q, mid, run_all)
            if pr == 0:
                owed = a_quarter(0, 1, 1, [owed])
            if pr == PAIRS - 1:
                owed = a_quarter(2, 1, 1, [owed])
                yq = [y_turn(*pend[0])]
                pend = pend[1:]
                pend.append((2 * pr, 0, h_step(pr, 0, [lambda: owed() and None], yq)))
            else:
                pend.append((2 * pr, 0, h_step(pr, 0)))
        with tc.manual_schedule():
            for pr in range(PAIRS):
                mid = []
                if len(pend) >= YLAG:
                    mid = [lambda item=pend[0]: y_turn(*item)]
                    pend = pend[1:]
                pend.append((2 * pr, 1, h_step(pr, 1, mid, last=(pr == PAIRS - 1))))
            for item in pend:
                y_turn(*item)()
            store_scales()
